import numpy as np
import ml_dtypes


def mxq(x, axis, fmt="e4m3"):
    dtype, down = {"e4m3": (ml_dtypes.float8_e4m3fn, 7), "e5m2": (ml_dtypes.float8_e5m2, 14)}[fmt]
    v = np.moveaxis(np.asarray(x, np.float32).astype(ml_dtypes.bfloat16).astype(np.float64), axis, -1)
    blocks = v.reshape(v.shape[:-1] + (-1, 32))
    amax = np.abs(blocks).max(-1, keepdims=True)
    byte = np.maximum(np.where(amax > 0, np.frexp(amax)[1] - 1 + 127, 0) - down, 1)
    scale = np.exp2(byte - 127.0)
    codes = (blocks / scale).astype(np.float32).astype(dtype).astype(np.float64)
    return np.moveaxis((codes * scale).reshape(v.shape), -1, axis)


WIDE = False


def mx_kscale(k):
    if not WIDE:
        return np.ones(k)
    levels = np.array([10, -10, 5, -5, 0])
    if k % 512:
        return np.exp2(np.random.permutation(np.resize(levels, k // 32))).repeat(32)
    a = np.empty((k // 512, 16))
    for p in range(k // 512):
        a[p, :8] = np.random.permutation(np.resize(levels, 8))
        for g in range(8):
            far = levels[np.abs(levels - a[p, g]) >= 10]
            a[p, g + 8] = far[np.random.randint(len(far))]
    return np.exp2(a.ravel()).repeat(32)


def f64(x):
    return np.asarray(x).astype(np.float64)


def striped(idx):
    return np.tile(idx.reshape(-1, 16).T, (8, 1)).astype(np.uint16)


def unstriped(offs):
    return offs[:16].T.reshape(-1).astype(np.int64)


def pack_weight(w):
    k, n = w.shape
    w = f64(np.asarray(w, np.float32).astype(ml_dtypes.bfloat16)).reshape(k // 32, 32, n)
    amax = np.abs(w).max(1)
    byte = np.clip(np.where(amax > 0, np.frexp(amax)[1] - 1 + 127 - 7, 1), 1, 254)
    scaled = (w * np.exp2(127.0 - byte)[:, None, :]).reshape(k, n).astype(np.float32)
    words = np.ascontiguousarray(scaled.reshape(k // 512, 128, 4, n).transpose(0, 1, 3, 2)).astype(ml_dtypes.float8_e4m3fn).view(np.uint8)
    return words, np.ascontiguousarray(byte.astype(np.uint8).reshape(k // 512, 16, n))


def unpack_weight(words, scales):
    g, p, n, _ = words.shape
    vals = np.ascontiguousarray(words).view(ml_dtypes.float8_e4m3fn).astype(np.float64) * np.repeat(np.exp2(scales.astype(np.float64) - 127.0), 8, axis=1)[..., None]
    return vals.transpose(0, 1, 3, 2).reshape(g * 512, n)


def gelu(v):
    return 0.5 * v * (1.0 + np.tanh(np.sqrt(2.0 / np.pi) * (v + 0.044715 * v**3)))


K, T, S, H, N = 1024, 2048, 1024, 512, 128
P = 2 ** 7


def setup_inputs():
    n = np.random.standard_normal
    s = mx_kscale(K)[:, None]
    u = mx_kscale(H)
    packed_xT = pack_weight(n((K, T)) * s)
    return {
        "x_words": packed_xT[0],
        "x_scales": packed_xT[1],
        "w1": (n((K, H)) / np.sqrt(K) / s * u).astype(np.float32),
        "w2": (n((H, N)) / np.sqrt(H) / u[:, None]).astype(np.float32),
        "share": np.tile(np.random.uniform(0.1, 0.9, S), (P, 1)).astype(np.float32),
        "offs": striped(np.random.permutation(T)[:S]),
        "par": striped(np.random.permutation(S)[(S * np.random.uniform(0, 1, S) ** 4).astype(np.int64)]),
    }


def reference(x_words, x_scales, w1, w2, share, offs, par):
    xq = unpack_weight(x_words, x_scales)[:, unstriped(offs)]
    h = gelu(mxq(f64(w1), 0, "e4m3").T @ xq)
    z = h + h[:, unstriped(par)] * f64(share)[:1]
    return mxq(f64(w2), 0, "e4m3").T @ mxq(z, 0, "e4m3")

@@ -1,0 +1,211 @@
+from contextlib import ExitStack
+
+import concourse.mybir as mybir
+from concourse.masks import make_identity
+
+K, T, S, H, N = 1024, 2048, 1024, 512, 128
+FLOPS = 2 * K * H * S + 2 * H * N * S
+
+F32 = mybir.dt.float32
+BF16 = mybir.dt.bfloat16
+I32 = mybir.dt.int32
+U32 = mybir.dt.uint32
+U16 = mybir.dt.uint16
+U8 = mybir.dt.uint8
+FP8X4 = mybir.dt.float8_e4m3fn_x4
+GELU = mybir.ActivationFunctionType.Gelu_apprx_tanh
+MULT = mybir.AluOpType.mult
+
+P = 128
+PACK = 4
+PASSES = K // (P * PACK)
+TILES = H // P
+HALF = S // 2
+QUARTER = S // 4
+LANES = 16
+
+
+def tile_picked_treeup_gelu_p_kernel(tc, x_words, x_scales, w1, w2, share, offs, par, out):
+    nc = tc.nc
+    with ExitStack() as ctx:
+        keep = ctx.enter_context(tc.tile_pool(name="keep", bufs=1))
+        ring = ctx.enter_context(tc.tile_pool(name="ring", bufs=2))
+        psum_u = ctx.enter_context(tc.psum_pool(name="psum_u", bufs=2))
+        psum_z = ctx.enter_context(tc.psum_pool(name="psum_z", bufs=3))
+        psum_w = ctx.enter_context(tc.psum_pool(name="psum_w", bufs=2))
+        psum_o = ctx.enter_context(tc.psum_pool(name="psum_o", bufs=1))
+
+        offs_sb = keep.tile([P, S // LANES], U16, name="offs_sb")
+        par_sb = keep.tile([P, S // LANES], U16, name="par_sb")
+        scale_table = keep.tile([P, T], U8, name="scale_table", align_bytes=64)
+        word_table = [keep.tile([P, T], I32, name="word_table%d" % z, align_bytes=64) for z in range(PASSES)]
+        identity = keep.tile([P, P], F32, name="identity")
+
+        nc.vector.memset(scale_table[:].bitcast(I32), 0)
+        for q in range(4):
+            nc.scalar.dma_start(
+                out=scale_table[32 * q : 32 * q + 4 * PASSES, :].bitcast(I32),
+                in_=x_scales[:, 4 * q : 4 * q + 4, :].bitcast(I32),
+            )
+        make_identity(nc, identity[:])
+
+        def load_words(z):
+            nc.sync.dma_start(out=word_table[z][:], in_=x_words[z].rearrange("p n t -> p (n t)").bitcast(I32))
+
+        w1_raw = {}
+
+        def load_w1(z, first, count):
+            raw = keep.tile([P, PACK, count * P], F32, name="w1_raw%d_%d" % (z, first))
+            rows = w1[z * P * PACK : (z + 1) * P * PACK, first * P : (first + count) * P]
+            nc.sync.dma_start(out=raw[:], in_=rows.rearrange("(p j) c -> p j c", j=PACK))
+            for t in range(count):
+                w1_raw[(z, first + t)] = raw[:, :, t * P : (t + 1) * P]
+
+        share_sb = [keep.tile([P, HALF], F32, name="share%d" % a) for a in range(2)]
+        w2_raw = keep.tile([P, PACK, N], F32, name="w2_raw")
+
+        nc.sync.dma_start(offs_sb[:], offs)
+        load_words(0)
+        load_w1(0, 0, 1)
+        load_words(1)
+        load_w1(1, 0, 1)
+        nc.sync.dma_start(par_sb[:], par)
+        nc.sync.dma_start(out=share_sb[0][:], in_=share[:, :HALF])
+        load_w1(0, 1, 1)
+        load_w1(1, 1, 1)
+        nc.sync.dma_start(out=share_sb[1][:], in_=share[:, HALF:])
+        load_w1(0, 2, 2)
+        load_w1(1, 2, 2)
+        nc.sync.dma_start(out=w2_raw[:], in_=w2.rearrange("(p j) m -> p j m", j=PACK))
+
+        def interleave(engine_copy, raw, name):
+            grouped = keep.tile([P, P, PACK], BF16, name=name, align_bytes=64)
+            engine_copy(
+                out=grouped[:].rearrange("p (c i) j -> p c j i", i=4),
+                in_=raw.rearrange("p j (c i) -> p c j i", i=4),
+            )
+            return grouped
+
+        def quantize(grouped, width, name):
+            codes = keep.tile([P, width], U32, name=name + "_codes", align_bytes=64)
+            scales = keep.tile([P, width], U8, name=name + "_scales", align_bytes=64)
+            nc.vector.quantize_mx(out=codes[:].bitcast(FP8X4), scales=scales[:], in_=grouped)
+            return codes, scales
+
+        w1_mx = {}
+
+        def prepare_w1(z, t):
+            grouped = interleave(nc.scalar.copy, w1_raw[(z, t)], "w1_bf%d_%d" % (z, t))
+            w1_mx[(z, t)] = quantize(grouped[:].rearrange("p c j -> p (c j)"), P, "w1_%d_%d" % (z, t))
+
+        x_scale = keep.tile([P, S], U8, name="x_scale", align_bytes=64)
+        x_code = [keep.tile([P, S], U32, name="x_code%d" % z, align_bytes=64) for z in range(PASSES)]
+
+        def lanes(a, b):
+            return slice(a // LANES, b // LANES)
+
+        def gather_words(z, a, b):
+            nc.vector.tensor_copy(x_code[z][:, a:b], word_table[z][:].bitcast(U32).indirect(offs_sb[:, lanes(a, b)]))
+
+        nc.vector.tensor_copy(x_scale[:], scale_table[:].indirect(offs_sb[:]))
+        gather_words(0, 0, S)
+        prepare_w1(0, 0)
+        gather_words(1, 0, HALF)
+        prepare_w1(1, 0)
+        gather_words(1, HALF, S)
+
+        h = [keep.tile([P, S], F32, name="h%d" % t) for t in range(TILES)]
+
+        def first_layer(t):
+            for a in range(2):
+                cols = slice(a * HALF, (a + 1) * HALF)
+                acc = psum_u.tile([P, HALF], F32, name="acc")
+                for z in range(PASSES):
+                    codes, scales = w1_mx[(z, t)]
+                    nc.tensor.matmul_mx(
+                        out=acc[:],
+                        lhsT=codes[:].bitcast(FP8X4),
+                        lhsT_scale=scales[:],
+                        rhs=x_code[z][:, cols].bitcast(FP8X4),
+                        rhs_scale=x_scale[4 * z : P, cols],
+                        start=(z == 0),
+                        stop=(z == PASSES - 1),
+                    )
+                nc.scalar.activation(out=h[t][:, cols], in_=acc[:], func=GELU)
+
+        blocks = QUARTER // P
+        z_rows = [keep.tile([P, blocks, 2, P, 2], BF16, name="z_rows%d" % c) for c in range(4)]
+
+        def mix(t, a, b):
+            width = b - a
+            taken = ring.tile([P, HALF], F32, name="taken")
+            nc.vector.tensor_tensor(
+                taken[:, :width],
+                h[t][:].indirect(par_sb[:, lanes(a, b)]),
+                share_sb[a // HALF][:, a % HALF : a % HALF + width],
+                MULT,
+            )
+            count = width // P
+            summed = psum_z.tile([P, HALF // P, P], F32, name="summed")
+            for n in range(count):
+                nc.tensor.matmul(summed[:, n, :], lhsT=h[t][:, a + n * P : a + (n + 1) * P], rhs=identity[:], start=(n == 0), stop=False, is_transpose=True)
+            for n in range(count):
+                nc.tensor.matmul(summed[:, n, :], lhsT=taken[:, n * P : (n + 1) * P], rhs=identity[:], start=False, stop=(n == count - 1), is_transpose=True)
+            for c in range(width // QUARTER):
+                nc.scalar.copy(
+                    out=z_rows[a // QUARTER + c][:, :, :, 32 * t : 32 * (t + 1), :],
+                    in_=summed[:, c * blocks : (c + 1) * blocks, :].rearrange("j n (r u e) -> j n u r e", u=2, e=2),
+                )
+
+        def second_layer(c):
+            words = z_rows[c][:].rearrange("j n u p e -> j (n u p e)").bitcast(F32)
+            turned = psum_w.tile([P, blocks, 2, P], F32, name="turned")
+            for n in range(blocks):
+                for u in range(2):
+                    at = (2 * n + u) * P
+                    nc.tensor.transpose(turned[:, n, u, :], words[:, at : at + P], identity[:])
+            grouped = ring.tile([P, QUARTER * PACK], BF16, name="z_bf", align_bytes=64)
+            nc.scalar.copy(
+                out=grouped[:].bitcast(F32).rearrange("p (n j u) -> p n j u", n=blocks, u=2),
+                in_=turned[:].rearrange("p n u j -> p n j u"),
+            )
+            codes, scales = quantize(grouped[:], QUARTER, "z%d" % c)
+            acc = psum_o.tile([P, QUARTER], F32, name="acc_out")
+            nc.tensor.matmul_mx(
+                out=acc[:],
+                lhsT=w2_mx[0][:].bitcast(FP8X4),
+                lhsT_scale=w2_mx[1][:],
+                rhs=codes[:].bitcast(FP8X4),
+                rhs_scale=scales[:],
+                start=True,
+                stop=True,
+            )
+            result = ring.tile([P, QUARTER], F32, name="result")
+            nc.scalar.copy(out=result[:], in_=acc[:])
+            nc.sync.dma_start(out=out[:, c * QUARTER : (c + 1) * QUARTER], in_=result[:])
+
+        first_layer(0)
+        for z in range(PASSES):
+            prepare_w1(z, 1)
+        mix(0, 0, HALF)
+        first_layer(1)
+        mix(0, HALF, S)
+        for z in range(PASSES):
+            prepare_w1(z, 2)
+        mix(1, 0, HALF)
+        first_layer(2)
+        for z in range(PASSES):
+            prepare_w1(z, 3)
+        mix(1, HALF, S)
+        first_layer(3)
+        w2_bf = interleave(nc.scalar.copy, w2_raw[:], "w2_bf")
+        w2_mx = quantize(w2_bf[:].rearrange("p c j -> p (c j)"), N, "w2")
+        mix(2, 0, HALF)
+        mix(3, 0, HALF)
+        mix(2, HALF, S)
+        second_layer(0)
+        second_layer(1)
+        mix(3, HALF, HALF + QUARTER)
+        mix(3, HALF + QUARTER, S)
+        second_layer(2)
+        second_layer(3)

@@ -21,32 +21,39 @@ PACK = 4
 PASSES = K // (P * PACK)
 TILES = H // P
 HALF = S // 2
-QUARTER = S // 4
 LANES = 16
+QUADRANTS = 4
+SCALE_ROWS = 4
+RUN = S // P
+BANK_BLOCKS = 4
+
+SPAN_A, SPAN_B, SPAN_C = (0, 512), (512, 896), (896, 1024)
+SPANS = [SPAN_A, SPAN_B, SPAN_C]
 
 
 def tile_picked_treeup_gelu_p_kernel(tc, x_words, x_scales, w1, w2, share, offs, par, out):
     nc = tc.nc
+    on_scalar, on_vector = nc.scalar.copy, nc.vector.tensor_copy
     with ExitStack() as ctx:
         keep = ctx.enter_context(tc.tile_pool(name="keep", bufs=1))
-        ring = ctx.enter_context(tc.tile_pool(name="ring", bufs=2))
-        psum_u = ctx.enter_context(tc.psum_pool(name="psum_u", bufs=2))
-        psum_z = ctx.enter_context(tc.psum_pool(name="psum_z", bufs=3))
-        psum_w = ctx.enter_context(tc.psum_pool(name="psum_w", bufs=2))
-        psum_o = ctx.enter_context(tc.psum_pool(name="psum_o", bufs=1))
+        reuse = ctx.enter_context(tc.tile_pool(name="reuse", bufs=1))
+        psum = ctx.enter_context(tc.psum_pool(name="psum", bufs=1))
+
+        def bank(shape, index):
+            return psum.tile(shape, F32, name="bank%d" % index, tag="bank%d" % index)
+
+        def lanes(a, b):
+            return slice(a // LANES, b // LANES)
 
         offs_sb = keep.tile([P, S // LANES], U16, name="offs_sb")
         par_sb = keep.tile([P, S // LANES], U16, name="par_sb")
         scale_table = keep.tile([P, T], U8, name="scale_table", align_bytes=64)
-        word_table = [keep.tile([P, T], I32, name="word_table%d" % z, align_bytes=64) for z in range(PASSES)]
+        word_table = [reuse.tile([P, T], I32, name="word_table%d" % z, tag="word_table%d" % z, align_bytes=64) for z in range(PASSES)]
         identity = keep.tile([P, P], F32, name="identity")
+        share_runs = keep.tile([P, RUN], F32, name="share_runs")
+        w2_raw = keep.tile([P, PACK, N], F32, name="w2_raw")
 
         nc.vector.memset(scale_table[:].bitcast(I32), 0)
-        for q in range(4):
-            nc.scalar.dma_start(
-                out=scale_table[32 * q : 32 * q + 4 * PASSES, :].bitcast(I32),
-                in_=x_scales[:, 4 * q : 4 * q + 4, :].bitcast(I32),
-            )
         make_identity(nc, identity[:])
 
         def load_words(z):
@@ -55,36 +62,43 @@ def tile_picked_treeup_gelu_p_kernel(tc, x_words, x_scales, w1, w2, share, offs,
         w1_raw = {}
 
         def load_w1(z, first, count):
-            raw = keep.tile([P, PACK, count * P], F32, name="w1_raw%d_%d" % (z, first))
+            raw = keep.tile([P, PACK, count * P], F32, name="w1_raw%d_%d" % (z, first), align_bytes=64)
             rows = w1[z * P * PACK : (z + 1) * P * PACK, first * P : (first + count) * P]
             nc.sync.dma_start(out=raw[:], in_=rows.rearrange("(p j) c -> p j c", j=PACK))
-            for t in range(count):
-                w1_raw[(z, first + t)] = raw[:, :, t * P : (t + 1) * P]
-
-        share_sb = [keep.tile([P, HALF], F32, name="share%d" % a) for a in range(2)]
-        w2_raw = keep.tile([P, PACK, N], F32, name="w2_raw")
+            for t in range(first, first + count):
+                w1_raw[(z, t)] = (raw, (t - first) * P)
 
         nc.sync.dma_start(offs_sb[:], offs)
         load_words(0)
-        load_w1(0, 0, 1)
-        load_words(1)
-        load_w1(1, 0, 1)
         nc.sync.dma_start(par_sb[:], par)
-        nc.sync.dma_start(out=share_sb[0][:], in_=share[:, :HALF])
-        load_w1(0, 1, 1)
-        load_w1(1, 1, 1)
-        nc.sync.dma_start(out=share_sb[1][:], in_=share[:, HALF:])
-        load_w1(0, 2, 2)
-        load_w1(1, 2, 2)
+        nc.sync.dma_start(out=share_runs[:], in_=share[0:1, :].rearrange("o (p c) -> (o p) c", c=RUN))
+        for q in range(QUADRANTS):
+            nc.sync.dma_start(
+                out=scale_table[32 * q : 32 * q + SCALE_ROWS * PASSES, :].bitcast(I32),
+                in_=x_scales[:, SCALE_ROWS * q : SCALE_ROWS * (q + 1), :].bitcast(I32),
+            )
+        load_w1(0, 0, TILES)
+        load_words(1)
+        load_w1(1, 0, 2)
         nc.sync.dma_start(out=w2_raw[:], in_=w2.rearrange("(p j) m -> p j m", j=PACK))
+        load_w1(1, 2, 2)
 
-        def interleave(engine_copy, raw, name):
-            grouped = keep.tile([P, P, PACK], BF16, name=name, align_bytes=64)
+        spread = [bank([P, BANK_BLOCKS, P], b) for b in range(RUN // BANK_BLOCKS)]
+        for c in range(RUN):
+            nc.tensor.transpose(spread[c // BANK_BLOCKS][:, c % BANK_BLOCKS, :], share_runs[:, c : c + 1].to_broadcast([P, P]), identity[:])
+        share_sb = {a: reuse.tile([P, b - a], F32, name="share%d" % a, tag="share%d" % a, align_bytes=64) for a, b in SPANS}
+        for s in range(len(spread)):
+            for a, b in SPANS:
+                on_scalar(
+                    out=share_sb[a][:].rearrange("p (n s c) -> p n s c", s=len(spread), c=BANK_BLOCKS)[:, :, s, :],
+                    in_=spread[s][:, :, a // RUN : b // RUN].rearrange("p c n -> p n c"),
+                )
+
+        def interleave(engine_copy, raw, grouped):
             engine_copy(
-                out=grouped[:].rearrange("p (c i) j -> p c j i", i=4),
+                out=grouped.rearrange("p (c i) j -> p c j i", i=4),
                 in_=raw.rearrange("p j (c i) -> p c j i", i=4),
             )
-            return grouped
 
         def quantize(grouped, width, name):
             codes = keep.tile([P, width], U32, name=name + "_codes", align_bytes=64)
@@ -92,120 +106,148 @@ def tile_picked_treeup_gelu_p_kernel(tc, x_words, x_scales, w1, w2, share, offs,
             nc.vector.quantize_mx(out=codes[:].bitcast(FP8X4), scales=scales[:], in_=grouped)
             return codes, scales
 
+        w1_bf = {}
         w1_mx = {}
 
-        def prepare_w1(z, t):
-            grouped = interleave(nc.scalar.copy, w1_raw[(z, t)], "w1_bf%d_%d" % (z, t))
-            w1_mx[(z, t)] = quantize(grouped[:].rearrange("p c j -> p (c j)"), P, "w1_%d_%d" % (z, t))
+        def round_w1(engine_copy, z, first, count, tag):
+            grouped = reuse.tile([P, count * P, PACK], BF16, name="w1_bf%d_%d" % (z, first), tag=tag, align_bytes=64)
+            raw, at = w1_raw[(z, first)]
+            interleave(engine_copy, raw[:, :, at : at + count * P], grouped[:])
+            w1_bf[(z, first)] = (grouped, count)
+
+        def quantize_w1(z, first):
+            grouped, count = w1_bf[(z, first)]
+            codes, scales = quantize(grouped[:].rearrange("p c j -> p (c j)"), count * P, "w1_%d_%d" % (z, first))
+            for t in range(count):
+                w1_mx[(z, first + t)] = (codes[:, t * P : (t + 1) * P], scales[:, t * P : (t + 1) * P])
 
         x_scale = keep.tile([P, S], U8, name="x_scale", align_bytes=64)
-        x_code = [keep.tile([P, S], U32, name="x_code%d" % z, align_bytes=64) for z in range(PASSES)]
+        x_code = {}
 
-        def lanes(a, b):
-            return slice(a // LANES, b // LANES)
-
-        def gather_words(z, a, b):
-            nc.vector.tensor_copy(x_code[z][:, a:b], word_table[z][:].bitcast(U32).indirect(offs_sb[:, lanes(a, b)]))
-
-        nc.vector.tensor_copy(x_scale[:], scale_table[:].indirect(offs_sb[:]))
-        gather_words(0, 0, S)
-        prepare_w1(0, 0)
-        gather_words(1, 0, HALF)
-        prepare_w1(1, 0)
-        gather_words(1, HALF, S)
+        def gather_words(z, a, b, tag):
+            picked = reuse.tile([P, b - a], U32, name="x_code%d_%d" % (z, a), tag=tag, align_bytes=64)
+            nc.vector.tensor_copy(picked[:], word_table[z][:].bitcast(U32).indirect(offs_sb[:, lanes(a, b)]))
+            for at in range(a, b, HALF):
+                x_code[(z, at)] = picked[:, at - a : at - a + HALF]
 
         h = [keep.tile([P, S], F32, name="h%d" % t) for t in range(TILES)]
 
         def first_layer(t):
-            for a in range(2):
-                cols = slice(a * HALF, (a + 1) * HALF)
-                acc = psum_u.tile([P, HALF], F32, name="acc")
+            for half in range(2):
+                a = half * HALF
+                acc = bank([P, HALF], 2 + (2 * t + half) % 4)
                 for z in range(PASSES):
                     codes, scales = w1_mx[(z, t)]
                     nc.tensor.matmul_mx(
                         out=acc[:],
-                        lhsT=codes[:].bitcast(FP8X4),
-                        lhsT_scale=scales[:],
-                        rhs=x_code[z][:, cols].bitcast(FP8X4),
-                        rhs_scale=x_scale[4 * z : P, cols],
+                        lhsT=codes.bitcast(FP8X4),
+                        lhsT_scale=scales,
+                        rhs=x_code[(z, a)].bitcast(FP8X4),
+                        rhs_scale=x_scale[SCALE_ROWS * z : P, a : a + HALF],
                         start=(z == 0),
                         stop=(z == PASSES - 1),
                     )
-                nc.scalar.activation(out=h[t][:, cols], in_=acc[:], func=GELU)
+                nc.scalar.activation(out=h[t][:, a : a + HALF], in_=acc[:], func=GELU)
 
-        blocks = QUARTER // P
-        z_rows = [keep.tile([P, blocks, 2, P, 2], BF16, name="z_rows%d" % c) for c in range(4)]
+        z_rows = {a: keep.tile([P, (b - a) // P, 2, P, 2], BF16, name="z_rows%d" % a, align_bytes=64) for a, b in SPANS}
 
-        def mix(t, a, b):
-            width = b - a
-            taken = ring.tile([P, HALF], F32, name="taken")
-            nc.vector.tensor_tensor(
-                taken[:, :width],
-                h[t][:].indirect(par_sb[:, lanes(a, b)]),
-                share_sb[a // HALF][:, a % HALF : a % HALF + width],
-                MULT,
-            )
-            count = width // P
-            summed = psum_z.tile([P, HALF // P, P], F32, name="summed")
-            for n in range(count):
-                nc.tensor.matmul(summed[:, n, :], lhsT=h[t][:, a + n * P : a + (n + 1) * P], rhs=identity[:], start=(n == 0), stop=False, is_transpose=True)
-            for n in range(count):
-                nc.tensor.matmul(summed[:, n, :], lhsT=taken[:, n * P : (n + 1) * P], rhs=identity[:], start=False, stop=(n == count - 1), is_transpose=True)
-            for c in range(width // QUARTER):
-                nc.scalar.copy(
-                    out=z_rows[a // QUARTER + c][:, :, :, 32 * t : 32 * (t + 1), :],
-                    in_=summed[:, c * blocks : (c + 1) * blocks, :].rearrange("j n (r u e) -> j n u r e", u=2, e=2),
-                )
-
-        def second_layer(c):
-            words = z_rows[c][:].rearrange("j n u p e -> j (n u p e)").bitcast(F32)
-            turned = psum_w.tile([P, blocks, 2, P], F32, name="turned")
-            for n in range(blocks):
-                for u in range(2):
-                    at = (2 * n + u) * P
-                    nc.tensor.transpose(turned[:, n, u, :], words[:, at : at + P], identity[:])
-            grouped = ring.tile([P, QUARTER * PACK], BF16, name="z_bf", align_bytes=64)
-            nc.scalar.copy(
-                out=grouped[:].bitcast(F32).rearrange("p (n j u) -> p n j u", n=blocks, u=2),
-                in_=turned[:].rearrange("p n u j -> p n j u"),
-            )
-            codes, scales = quantize(grouped[:], QUARTER, "z%d" % c)
-            acc = psum_o.tile([P, QUARTER], F32, name="acc_out")
-            nc.tensor.matmul_mx(
-                out=acc[:],
-                lhsT=w2_mx[0][:].bitcast(FP8X4),
-                lhsT_scale=w2_mx[1][:],
-                rhs=codes[:].bitcast(FP8X4),
-                rhs_scale=scales[:],
-                start=True,
-                stop=True,
-            )
-            result = ring.tile([P, QUARTER], F32, name="result")
-            nc.scalar.copy(out=result[:], in_=acc[:])
-            nc.sync.dma_start(out=out[:, c * QUARTER : (c + 1) * QUARTER], in_=result[:])
-
+        gather_words(0, 0, S, "x0")
+        nc.vector.tensor_copy(x_scale[:], scale_table[:].indirect(offs_sb[:]))
+        round_w1(on_scalar, 0, 0, 2, "bf00")
+        round_w1(on_scalar, 0, 2, 2, "bf02")
+        quantize_w1(0, 0)
+        gather_words(1, 0, HALF, "x1")
+        quantize_w1(0, 2)
+        round_w1(on_scalar, 1, 0, 1, "bf10")
+        round_w1(on_scalar, 1, 1, 1, "bf11")
+        quantize_w1(1, 0)
+        gather_words(1, HALF, S, "bf10")
+        quantize_w1(1, 1)
+        w2_bf = keep.tile([P, N, PACK], BF16, name="w2_bf", align_bytes=64)
+        interleave(on_scalar, w2_raw[:], w2_bf[:])
         first_layer(0)
-        for z in range(PASSES):
-            prepare_w1(z, 1)
-        mix(0, 0, HALF)
-        first_layer(1)
-        mix(0, HALF, S)
-        for z in range(PASSES):
-            prepare_w1(z, 2)
-        mix(1, 0, HALF)
-        first_layer(2)
-        for z in range(PASSES):
-            prepare_w1(z, 3)
-        mix(1, HALF, S)
-        first_layer(3)
-        w2_bf = interleave(nc.scalar.copy, w2_raw[:], "w2_bf")
-        w2_mx = quantize(w2_bf[:].rearrange("p c j -> p (c j)"), N, "w2")
-        mix(2, 0, HALF)
-        mix(3, 0, HALF)
-        mix(2, HALF, S)
-        second_layer(0)
-        second_layer(1)
-        mix(3, HALF, HALF + QUARTER)
-        mix(3, HALF + QUARTER, S)
-        second_layer(2)
-        second_layer(3)
+        round_w1(on_vector, 1, 2, 2, "word_table1")
+        quantize_w1(1, 2)
+        w2_codes, w2_scales = quantize(w2_bf[:].rearrange("p c j -> p (c j)"), N, "w2")
+        for t in range(1, TILES):
+            first_layer(t)
+
+        taken_tags = {SPAN_A: "word_table1", SPAN_B: "share%d" % SPAN_A[0], SPAN_C: "share%d" % SPAN_B[0]}
+        taken = {}
+
+        def take(t, span):
+            a, b = span
+            if t == 0:
+                taken[span] = reuse.tile([P, TILES * (b - a)], F32, name="taken%d" % a, tag=taken_tags[span], align_bytes=64)
+            product = taken[span][:, t * (b - a) : (t + 1) * (b - a)]
+            nc.vector.tensor_tensor(product, h[t][:].indirect(par_sb[:, lanes(a, b)]), share_sb[a][:], MULT)
+            return product
+
+        def mix(first, count, span, index, engine_copy):
+            a, b = span
+            blocks = (b - a) // P
+            summed = bank([P, blocks, count, P], index)
+            for t in range(count):
+                for n in range(blocks):
+                    nodes = slice(a + n * P, a + (n + 1) * P)
+                    nc.tensor.matmul(summed[:, n, t, :], lhsT=h[first + t][:, nodes], rhs=identity[:], start=(t == 0 and n == 0), stop=False, is_transpose=True)
+            for t in range(count):
+                product = take(first + t, span)
+                for n in range(blocks):
+                    is_last = t == count - 1 and n == blocks - 1
+                    nc.tensor.matmul(summed[:, n, t, :], lhsT=product[:, n * P : (n + 1) * P], rhs=identity[:], start=False, stop=is_last, is_transpose=True)
+            engine_copy(
+                out=z_rows[a][:, :, :, 32 * first : 32 * (first + count), :],
+                in_=summed[:].rearrange("j n t (r u e) -> j n u (t r) e", u=2, e=2),
+            )
+
+        def turn_back(span, engine_copy, turn_banks):
+            a, b = span
+            words = z_rows[a][:].rearrange("j n u p e -> j (n u p e)").bitcast(F32)
+            grouped = keep.tile([P, (b - a) * PACK], BF16, name="z_bf%d" % a, align_bytes=64)
+            for c, index in enumerate(turn_banks):
+                blocks = min(2, (b - a) // P - 2 * c)
+                turned = bank([P, blocks, 2, P], index)
+                for n in range(blocks):
+                    for u in range(2):
+                        at = (2 * (2 * c + n) + u) * P
+                        nc.tensor.transpose(turned[:, n, u, :], words[:, at : at + P], identity[:])
+                engine_copy(
+                    out=grouped[:, 2 * c * P * PACK : (2 * c + blocks) * P * PACK].bitcast(F32).rearrange("p (n j u) -> p n j u", n=blocks, u=2),
+                    in_=turned[:].rearrange("p n u j -> p n j u"),
+                )
+            return grouped
+
+        def second_layer(span, grouped, widths, index):
+            a, b = span
+            acc = bank([P, b - a], index)
+            at = 0
+            for width in widths:
+                codes, scales = quantize(grouped[:, at * PACK : (at + width) * PACK], width, "z%d" % (a + at))
+                nc.tensor.matmul_mx(
+                    out=acc[:, at : at + width],
+                    lhsT=w2_codes[:].bitcast(FP8X4),
+                    lhsT_scale=w2_scales[:],
+                    rhs=codes[:].bitcast(FP8X4),
+                    rhs_scale=scales[:],
+                    start=True,
+                    stop=True,
+                )
+                at = at + width
+            result = keep.tile([P, b - a], F32, name="result%d" % a)
+            on_scalar(out=result[:], in_=acc[:])
+            nc.sync.dma_start(out=out[:, a:b], in_=result[:])
+
+        for t in range(TILES):
+            mix(t, 1, SPAN_A, (6 + t) % 8, on_scalar)
+        mix(0, 1, SPAN_B, 2, on_scalar)
+        z_a = turn_back(SPAN_A, on_scalar, [3, 4])
+        mix(1, 1, SPAN_B, 1, on_scalar)
+        mix(2, 1, SPAN_B, 2, on_scalar)
+        mix(3, 1, SPAN_B, 3, on_scalar)
+        z_b = turn_back(SPAN_B, on_scalar, [6, 7])
+        mix(0, 3, SPAN_C, 1, on_vector)
+        mix(3, 1, SPAN_C, 2, on_vector)
+        second_layer(SPAN_A, z_a, [512], 1)
+        second_layer(SPAN_B, z_b, [256, 128], 5)
+        second_layer(SPAN_C, turn_back(SPAN_C, on_vector, [4]), [128], 0)

@@ -80,8 +80,11 @@ def tile_picked_treeup_gelu_p_kernel(tc, x_words, x_scales, w1, w2, share, offs,
         load_w1(0, 0, TILES)
         load_words(1)
         load_w1(1, 0, 2)
-        nc.sync.dma_start(out=w2_raw[:], in_=w2.rearrange("(p j) m -> p j m", j=PACK))
         load_w1(1, 2, 2)
+        nc.sync.dma_start(out=w2_raw[:], in_=w2.rearrange("(p j) m -> p j m", j=PACK))
+
+        warm = keep.tile([P, 1], F32, name="warm")
+        nc.scalar.activation(out=warm[:], in_=share_runs[:, 0:1], func=GELU)
 
         spread = [bank([P, BANK_BLOCKS, P], b) for b in range(RUN // BANK_BLOCKS)]
         for c in range(RUN):
@@ -163,14 +166,14 @@ def tile_picked_treeup_gelu_p_kernel(tc, x_words, x_scales, w1, w2, share, offs,
         quantize_w1(1, 0)
         gather_words(1, HALF, S, "bf10")
         quantize_w1(1, 1)
-        w2_bf = keep.tile([P, N, PACK], BF16, name="w2_bf", align_bytes=64)
-        interleave(on_scalar, w2_raw[:], w2_bf[:])
         first_layer(0)
         round_w1(on_vector, 1, 2, 2, "word_table1")
         quantize_w1(1, 2)
-        w2_codes, w2_scales = quantize(w2_bf[:].rearrange("p c j -> p (c j)"), N, "w2")
         for t in range(1, TILES):
             first_layer(t)
+        w2_bf = reuse.tile([P, N, PACK], BF16, name="w2_bf", tag="x0", align_bytes=64)
+        interleave(on_scalar, w2_raw[:], w2_bf[:])
+        w2_codes, w2_scales = quantize(w2_bf[:].rearrange("p c j -> p (c j)"), N, "w2")
 
         taken_tags = {SPAN_A: "word_table1", SPAN_B: "share%d" % SPAN_A[0], SPAN_C: "share%d" % SPAN_B[0]}
         taken = {}

from contextlib import ExitStack

import concourse.mybir as mybir
from concourse.masks import make_identity

K, T, S, H, N = 1024, 2048, 1024, 512, 128
FLOPS = 2 * K * H * S + 2 * H * N * S

F32 = mybir.dt.float32
BF16 = mybir.dt.bfloat16
I32 = mybir.dt.int32
U32 = mybir.dt.uint32
U16 = mybir.dt.uint16
U8 = mybir.dt.uint8
FP8X4 = mybir.dt.float8_e4m3fn_x4
GELU = mybir.ActivationFunctionType.Gelu_apprx_tanh
MULT = mybir.AluOpType.mult

P = 128
PACK = 4
PASSES = K // (P * PACK)
TILES = H // P
HALF = S // 2
LANES = 16
QUADRANTS = 4
SCALE_ROWS = 4
RUN = S // P
BANK_BLOCKS = 4

SPAN_A, SPAN_B, SPAN_C = (0, 512), (512, 896), (896, 1024)
SPANS = [SPAN_A, SPAN_B, SPAN_C]


def tile_picked_treeup_gelu_p_kernel(tc, x_words, x_scales, w1, w2, share, offs, par, out):
    nc = tc.nc
    on_scalar, on_vector = nc.scalar.copy, nc.vector.tensor_copy
    with ExitStack() as ctx:
        keep = ctx.enter_context(tc.tile_pool(name="keep", bufs=1))
        reuse = ctx.enter_context(tc.tile_pool(name="reuse", bufs=1))
        psum = ctx.enter_context(tc.psum_pool(name="psum", bufs=1))

        def bank(shape, index):
            return psum.tile(shape, F32, name="bank%d" % index, tag="bank%d" % index)

        def lanes(a, b):
            return slice(a // LANES, b // LANES)

        offs_sb = keep.tile([P, S // LANES], U16, name="offs_sb")
        par_sb = keep.tile([P, S // LANES], U16, name="par_sb")
        scale_table = keep.tile([P, T], U8, name="scale_table", align_bytes=64)
        word_table = [reuse.tile([P, T], I32, name="word_table%d" % z, tag="word_table%d" % z, align_bytes=64) for z in range(PASSES)]
        identity = keep.tile([P, P], F32, name="identity")
        share_runs = keep.tile([P, RUN], F32, name="share_runs")
        w2_raw = keep.tile([P, PACK, N], F32, name="w2_raw")

        nc.vector.memset(scale_table[:].bitcast(I32), 0)
        make_identity(nc, identity[:])

        def load_words(z):
            nc.sync.dma_start(out=word_table[z][:], in_=x_words[z].rearrange("p n t -> p (n t)").bitcast(I32))

        w1_raw = {}

        def load_w1(z, first, count):
            raw = keep.tile([P, PACK, count * P], F32, name="w1_raw%d_%d" % (z, first), align_bytes=64)
            rows = w1[z * P * PACK : (z + 1) * P * PACK, first * P : (first + count) * P]
            nc.sync.dma_start(out=raw[:], in_=rows.rearrange("(p j) c -> p j c", j=PACK))
            for t in range(first, first + count):
                w1_raw[(z, t)] = (raw, (t - first) * P)

        nc.sync.dma_start(offs_sb[:], offs)
        load_words(0)
        nc.sync.dma_start(par_sb[:], par)
        nc.sync.dma_start(out=share_runs[:], in_=share[0:1, :].rearrange("o (p c) -> (o p) c", c=RUN))
        for q in range(QUADRANTS):
            nc.sync.dma_start(
                out=scale_table[32 * q : 32 * q + SCALE_ROWS * PASSES, :].bitcast(I32),
                in_=x_scales[:, SCALE_ROWS * q : SCALE_ROWS * (q + 1), :].bitcast(I32),
            )
        load_w1(0, 0, TILES)
        load_words(1)
        load_w1(1, 0, 2)
        load_w1(1, 2, 2)
        nc.sync.dma_start(out=w2_raw[:], in_=w2.rearrange("(p j) m -> p j m", j=PACK))

        warm = keep.tile([P, 1], F32, name="warm")
        nc.scalar.activation(out=warm[:], in_=share_runs[:, 0:1], func=GELU)

        spread = [bank([P, BANK_BLOCKS, P], b) for b in range(RUN // BANK_BLOCKS)]
        for c in range(RUN):
            nc.tensor.transpose(spread[c // BANK_BLOCKS][:, c % BANK_BLOCKS, :], share_runs[:, c : c + 1].to_broadcast([P, P]), identity[:])
        share_sb = {a: reuse.tile([P, b - a], F32, name="share%d" % a, tag="share%d" % a, align_bytes=64) for a, b in SPANS}
        for s in range(len(spread)):
            for a, b in SPANS:
                on_scalar(
                    out=share_sb[a][:].rearrange("p (n s c) -> p n s c", s=len(spread), c=BANK_BLOCKS)[:, :, s, :],
                    in_=spread[s][:, :, a // RUN : b // RUN].rearrange("p c n -> p n c"),
                )

        def interleave(engine_copy, raw, grouped):
            engine_copy(
                out=grouped.rearrange("p (c i) j -> p c j i", i=4),
                in_=raw.rearrange("p j (c i) -> p c j i", i=4),
            )

        def quantize(grouped, width, name):
            codes = keep.tile([P, width], U32, name=name + "_codes", align_bytes=64)
            scales = keep.tile([P, width], U8, name=name + "_scales", align_bytes=64)
            nc.vector.quantize_mx(out=codes[:].bitcast(FP8X4), scales=scales[:], in_=grouped)
            return codes, scales

        w1_bf = {}
        w1_mx = {}

        def round_w1(engine_copy, z, first, count, tag):
            grouped = reuse.tile([P, count * P, PACK], BF16, name="w1_bf%d_%d" % (z, first), tag=tag, align_bytes=64)
            raw, at = w1_raw[(z, first)]
            interleave(engine_copy, raw[:, :, at : at + count * P], grouped[:])
            w1_bf[(z, first)] = (grouped, count)

        def quantize_w1(z, first):
            grouped, count = w1_bf[(z, first)]
            codes, scales = quantize(grouped[:].rearrange("p c j -> p (c j)"), count * P, "w1_%d_%d" % (z, first))
            for t in range(count):
                w1_mx[(z, first + t)] = (codes[:, t * P : (t + 1) * P], scales[:, t * P : (t + 1) * P])

        x_scale = keep.tile([P, S], U8, name="x_scale", align_bytes=64)
        x_code = {}

        def gather_words(z, a, b, tag):
            picked = reuse.tile([P, b - a], U32, name="x_code%d_%d" % (z, a), tag=tag, align_bytes=64)
            nc.vector.tensor_copy(picked[:], word_table[z][:].bitcast(U32).indirect(offs_sb[:, lanes(a, b)]))
            for at in range(a, b, HALF):
                x_code[(z, at)] = picked[:, at - a : at - a + HALF]

        h = [keep.tile([P, S], F32, name="h%d" % t) for t in range(TILES)]

        def first_layer(t):
            for half in range(2):
                a = half * HALF
                acc = bank([P, HALF], 2 + (2 * t + half) % 4)
                for z in range(PASSES):
                    codes, scales = w1_mx[(z, t)]
                    nc.tensor.matmul_mx(
                        out=acc[:],
                        lhsT=codes.bitcast(FP8X4),
                        lhsT_scale=scales,
                        rhs=x_code[(z, a)].bitcast(FP8X4),
                        rhs_scale=x_scale[SCALE_ROWS * z : P, a : a + HALF],
                        start=(z == 0),
                        stop=(z == PASSES - 1),
                    )
                nc.scalar.activation(out=h[t][:, a : a + HALF], in_=acc[:], func=GELU)

        z_rows = {a: keep.tile([P, (b - a) // P, 2, P, 2], BF16, name="z_rows%d" % a, align_bytes=64) for a, b in SPANS}

        gather_words(0, 0, S, "x0")
        nc.vector.tensor_copy(x_scale[:], scale_table[:].indirect(offs_sb[:]))
        round_w1(on_scalar, 0, 0, 2, "bf00")
        round_w1(on_scalar, 0, 2, 2, "bf02")
        quantize_w1(0, 0)
        gather_words(1, 0, HALF, "x1")
        quantize_w1(0, 2)
        round_w1(on_scalar, 1, 0, 1, "bf10")
        round_w1(on_scalar, 1, 1, 1, "bf11")
        quantize_w1(1, 0)
        gather_words(1, HALF, S, "bf10")
        quantize_w1(1, 1)
        first_layer(0)
        round_w1(on_vector, 1, 2, 2, "word_table1")
        quantize_w1(1, 2)
        for t in range(1, TILES):
            first_layer(t)
        w2_bf = reuse.tile([P, N, PACK], BF16, name="w2_bf", tag="x0", align_bytes=64)
        interleave(on_scalar, w2_raw[:], w2_bf[:])
        w2_codes, w2_scales = quantize(w2_bf[:].rearrange("p c j -> p (c j)"), N, "w2")

        taken_tags = {SPAN_A: "word_table1", SPAN_B: "share%d" % SPAN_A[0], SPAN_C: "share%d" % SPAN_B[0]}
        taken = {}

        def take(t, span):
            a, b = span
            if t == 0:
                taken[span] = reuse.tile([P, TILES * (b - a)], F32, name="taken%d" % a, tag=taken_tags[span], align_bytes=64)
            product = taken[span][:, t * (b - a) : (t + 1) * (b - a)]
            nc.vector.tensor_tensor(product, h[t][:].indirect(par_sb[:, lanes(a, b)]), share_sb[a][:], MULT)
            return product

        def mix(first, count, span, index, engine_copy):
            a, b = span
            blocks = (b - a) // P
            summed = bank([P, blocks, count, P], index)
            for t in range(count):
                for n in range(blocks):
                    nodes = slice(a + n * P, a + (n + 1) * P)
                    nc.tensor.matmul(summed[:, n, t, :], lhsT=h[first + t][:, nodes], rhs=identity[:], start=(t == 0 and n == 0), stop=False, is_transpose=True)
            for t in range(count):
                product = take(first + t, span)
                for n in range(blocks):
                    is_last = t == count - 1 and n == blocks - 1
                    nc.tensor.matmul(summed[:, n, t, :], lhsT=product[:, n * P : (n + 1) * P], rhs=identity[:], start=False, stop=is_last, is_transpose=True)
            engine_copy(
                out=z_rows[a][:, :, :, 32 * first : 32 * (first + count), :],
                in_=summed[:].rearrange("j n t (r u e) -> j n u (t r) e", u=2, e=2),
            )

        def turn_back(span, engine_copy, turn_banks):
            a, b = span
            words = z_rows[a][:].rearrange("j n u p e -> j (n u p e)").bitcast(F32)
            grouped = keep.tile([P, (b - a) * PACK], BF16, name="z_bf%d" % a, align_bytes=64)
            for c, index in enumerate(turn_banks):
                blocks = min(2, (b - a) // P - 2 * c)
                turned = bank([P, blocks, 2, P], index)
                for n in range(blocks):
                    for u in range(2):
                        at = (2 * (2 * c + n) + u) * P
                        nc.tensor.transpose(turned[:, n, u, :], words[:, at : at + P], identity[:])
                engine_copy(
                    out=grouped[:, 2 * c * P * PACK : (2 * c + blocks) * P * PACK].bitcast(F32).rearrange("p (n j u) -> p n j u", n=blocks, u=2),
                    in_=turned[:].rearrange("p n u j -> p n j u"),
                )
            return grouped

        def second_layer(span, grouped, widths, index):
            a, b = span
            acc = bank([P, b - a], index)
            at = 0
            for width in widths:
                codes, scales = quantize(grouped[:, at * PACK : (at + width) * PACK], width, "z%d" % (a + at))
                nc.tensor.matmul_mx(
                    out=acc[:, at : at + width],
                    lhsT=w2_codes[:].bitcast(FP8X4),
                    lhsT_scale=w2_scales[:],
                    rhs=codes[:].bitcast(FP8X4),
                    rhs_scale=scales[:],
                    start=True,
                    stop=True,
                )
                at = at + width
            result = keep.tile([P, b - a], F32, name="result%d" % a)
            on_scalar(out=result[:], in_=acc[:])
            nc.sync.dma_start(out=out[:, a:b], in_=result[:])

        for t in range(TILES):
            mix(t, 1, SPAN_A, (6 + t) % 8, on_scalar)
        mix(0, 1, SPAN_B, 2, on_scalar)
        z_a = turn_back(SPAN_A, on_scalar, [3, 4])
        mix(1, 1, SPAN_B, 1, on_scalar)
        mix(2, 1, SPAN_B, 2, on_scalar)
        mix(3, 1, SPAN_B, 3, on_scalar)
        z_b = turn_back(SPAN_B, on_scalar, [6, 7])
        mix(0, 3, SPAN_C, 1, on_vector)
        mix(3, 1, SPAN_C, 2, on_vector)
        second_layer(SPAN_A, z_a, [512], 1)
        second_layer(SPAN_B, z_b, [256, 128], 5)
        second_layer(SPAN_C, turn_back(SPAN_C, on_vector, [4]), [128], 0)
